import numpy as np
import ml_dtypes


def mxq(x, axis, fmt="e4m3"):
    dtype, down = {"e4m3": (ml_dtypes.float8_e4m3fn, 7), "e5m2": (ml_dtypes.float8_e5m2, 14)}[fmt]
    v = np.moveaxis(np.asarray(x, np.float32).astype(ml_dtypes.bfloat16).astype(np.float64), axis, -1)
    blocks = v.reshape(v.shape[:-1] + (-1, 32))
    amax = np.abs(blocks).max(-1, keepdims=True)
    byte = np.maximum(np.where(amax > 0, np.frexp(amax)[1] - 1 + 127, 0) - down, 1)
    scale = np.exp2(byte - 127.0)
    codes = (blocks / scale).astype(np.float32).astype(dtype).astype(np.float64)
    return np.moveaxis((codes * scale).reshape(v.shape), -1, axis)


WIDE = False


def mx_kscale(k):
    if not WIDE:
        return np.ones(k)
    levels = np.array([10, -10, 5, -5, 0])
    if k % 512:
        return np.exp2(np.random.permutation(np.resize(levels, k // 32))).repeat(32)
    a = np.empty((k // 512, 16))
    for p in range(k // 512):
        a[p, :8] = np.random.permutation(np.resize(levels, 8))
        for g in range(8):
            far = levels[np.abs(levels - a[p, g]) >= 10]
            a[p, g + 8] = far[np.random.randint(len(far))]
    return np.exp2(a.ravel()).repeat(32)


def f64(x):
    return np.asarray(x).astype(np.float64)


def striped(idx):
    return np.tile(idx.reshape(-1, 16).T, (8, 1)).astype(np.uint16)


def unstriped(offs):
    return offs[:16].T.reshape(-1).astype(np.int64)


def striped8(idx):
    return np.concatenate([x.reshape(-1, 16).T for x in idx]).astype(np.uint16)


def runs(offs, k):
    lists = np.stack([offs[16 * r : 16 * r + 16].T.reshape(-1) for r in range(8)]).astype(np.int64)
    return lists[np.arange(k) % 512 // 64]


def pack_weight(w):
    k, n = w.shape
    w = f64(np.asarray(w, np.float32).astype(ml_dtypes.bfloat16)).reshape(k // 32, 32, n)
    amax = np.abs(w).max(1)
    byte = np.clip(np.where(amax > 0, np.frexp(amax)[1] - 1 + 127 - 7, 1), 1, 254)
    scaled = (w * np.exp2(127.0 - byte)[:, None, :]).reshape(k, n).astype(np.float32)
    words = np.ascontiguousarray(scaled.reshape(k // 512, 128, 4, n).transpose(0, 1, 3, 2)).astype(ml_dtypes.float8_e4m3fn).view(np.uint8)
    return words, np.ascontiguousarray(byte.astype(np.uint8).reshape(k // 512, 16, n))


def unpack_weight(words, scales):
    g, p, n, _ = words.shape
    vals = np.ascontiguousarray(words).view(ml_dtypes.float8_e4m3fn).astype(np.float64) * np.repeat(np.exp2(scales.astype(np.float64) - 127.0), 8, axis=1)[..., None]
    return vals.transpose(0, 1, 3, 2).reshape(g * 512, n)


K, T, S, N, H, W, C = 512, 2048, 256, 512, 512, 128, 512


def setup_inputs():
    n = np.random.standard_normal
    s = mx_kscale(K)[:, None]
    u = mx_kscale(K)
    packed_xT = pack_weight(n((K, T)) * s)
    perm = np.random.permutation(S)
    return {
        "x_words": packed_xT[0],
        "x_scales": packed_xT[1],
        "w1": (n((K, H)) / np.sqrt(K) / s).astype(np.float32),
        "w2": (n((K, H)) / np.sqrt(K) / s).astype(np.float32),
        "gn": (np.random.uniform(0.5, 1.5, (H, 1)) * u[:, None]).astype(np.float32),
        "w3": (n((H, N)) / np.sqrt(H) / u[:, None]).astype(np.float32),
        "gs": (np.random.uniform(0.5, 1.5, (K, 1)) / s).astype(np.float32),
        "offs": striped(np.random.permutation(T)[:S]),
        "two": striped(np.random.permutation(T)[:S]),
        "n1": striped8(np.stack([np.random.permutation(S) for _ in range(8)])),
        "n2": striped8(np.stack([np.random.permutation(S) for _ in range(8)])),
        "n3": striped8(np.stack([np.random.permutation(S) for _ in range(8)])),
        "n4": striped(perm[:W]),
        "n5": striped(perm[W:]),
        "cand": striped(np.random.permutation(T)[:C]),
        "n6": striped(np.random.permutation(S)[:W]),
        "n7": striped(np.random.permutation(S)[:W]),
    }


def reference(x_words, x_scales, w1, w2, gn, w3, gs, offs, two, n1, n2, n3, n4, n5, cand, n6, n7):
    x_cand = unpack_weight(x_words, x_scales)[:, unstriped(cand)]
    x_two = unpack_weight(x_words, x_scales)[:, unstriped(two)]
    d = mxq(f64(w2), 0, "e4m3").T @ x_two
    pa = d[:, unstriped(n4)]
    pb = d[:, unstriped(n5)]
    rb = pa * pb
    ra = pa + pb
    ds = np.zeros((H, S))
    ds[:, unstriped(n4)] = ra
    dt = ds.copy()
    dt[:, unstriped(n5)] = rb
    z2 = f64(gs) * dt
    b = 0.0625 * ((x_cand.T @ mxq(z2, 0, "e4m3")))
    xq = unpack_weight(x_words, x_scales)[:, unstriped(offs)]
    y = mxq(f64(w1), 0, "e4m3").T @ xq
    z = f64(gn) * (np.maximum(y, y[np.arange(H)[:, None], runs(n1, H)]) - (np.maximum(y[np.arange(H)[:, None], runs(n2, H)], y[np.arange(H)[:, None], runs(n3, H)])))
    a = mxq(f64(w3), 0, "e4m3").T @ mxq(z, 0, "e4m3")
    ra2 = b[:, unstriped(n7)] - (0.5 * a[:, unstriped(n6)])
    out = a.copy()
    out[:, unstriped(n6)] = ra2
    return out

@@ -1,0 +1,224 @@
+from contextlib import ExitStack
+
+import concourse.mybir as mybir
+
+F32 = mybir.dt.float32
+BF16 = mybir.dt.bfloat16
+I32 = mybir.dt.int32
+U32 = mybir.dt.uint32
+U16 = mybir.dt.uint16
+U8 = mybir.dt.uint8
+FP8X4 = mybir.dt.float8_e4m3fn_x4
+ALU = mybir.AluOpType
+COPY = mybir.ActivationFunctionType.Copy
+
+P = 128
+PACK = 4
+K = 512
+T = 2048
+S = 256
+W = 128
+C = 512
+HALF = K // 2
+FLOPS = 4 * 2 * K * K * S
+
+
+def tile_picked_tfcdputbmixbond_none_p_kernel(tc, x_words, x_scales, w1, w2, gn, w3, gs, offs, two, n1, n2, n3, n4, n5, cand, n6, n7, out):
+    nc = tc.nc
+    with ExitStack() as ctx:
+        keep = ctx.enter_context(tc.tile_pool(name="keep", bufs=1))
+        psum = ctx.enter_context(tc.psum_pool(name="psum", bufs=1))
+
+        def load_list(name, src):
+            tile = keep.tile(list(src.shape), U16, name=name)
+            nc.sync.dma_start(tile[:], src)
+            return tile
+
+        def load_half(name, w, h):
+            raw = keep.tile([P, PACK, HALF], F32, name=name, tag="reused_raw" if name == "w2_1" else name)
+            nc.sync.dma_start(raw[:], w.rearrange("(p j) c -> p j c", j=PACK)[:, :, h * HALF : (h + 1) * HALF])
+            return raw
+
+        def load_gain(name, g):
+            tile = keep.tile([P, PACK], F32, name=name)
+            nc.sync.dma_start(tile[:], g.rearrange("(p t) o -> p (t o)", t=PACK))
+            return tile
+
+        xs = keep.tile([P, T], U8, name="xs")
+        nc.gpsimd.memset(xs[:].bitcast(I32), 0)
+        xw = keep.tile([P, T], I32, name="xw")
+
+        l_offs = load_list("l_offs", offs)
+        l_two = load_list("l_two", two)
+        w1_raw = [load_half("w1_0", w1, 0)]
+        for q in range(4):
+            nc.sync.dma_start(xs[32 * q : 32 * q + 4, :].bitcast(I32), x_scales[0, 4 * q : 4 * q + 4, :].bitcast(I32))
+        w1_raw.append(load_half("w1_1", w1, 1))
+        l_cand = load_list("l_cand", cand)
+        nc.sync.dma_start(xw[:], x_words[0].rearrange("p c r -> p (c r)").bitcast(I32))
+        l_n1 = load_list("l_n1", n1)
+        l_n2 = load_list("l_n2", n2)
+        l_n3 = load_list("l_n3", n3)
+        gn_sb = load_gain("gn_sb", gn)
+        w2_raw = [load_half("w2_%d" % h, w2, h) for h in range(2)]
+        l_n4 = load_list("l_n4", n4)
+        l_n5 = load_list("l_n5", n5)
+        gs_sb = load_gain("gs_sb", gs)
+        w3_raw = [load_half("w3_%d" % h, w3, h) for h in range(2)]
+        l_n6 = load_list("l_n6", n6)
+        l_n7 = load_list("l_n7", n7)
+
+        def mx_tiles(name, width):
+            words = keep.tile([P, width], U32, name=name + "_words", align_bytes=64)
+            scales = keep.tile([P, width], U8, name=name + "_scales", align_bytes=64)
+            return words, scales
+
+        def pick_scales(picked, offsets):
+            nc.vector.tensor_copy(picked[1][:], xs[:].indirect(offsets[:]))
+
+        def pick_words(picked, offsets):
+            nc.vector.tensor_copy(picked[0][:], xw[:].bitcast(U32).indirect(offsets[:]))
+
+        def deal_half(copy, grouped, raw, h):
+            m = HALF // PACK
+            dst = grouped[:].rearrange("p (t m j) -> p m t j", t=PACK, j=PACK)[:, h * m : (h + 1) * m, :, :]
+            copy(dst, raw[:].rearrange("p j (m t) -> p m t j", t=PACK))
+
+        def weave_half(copy, grouped, raw, h):
+            n = HALF // PACK
+            dst = grouped[:].rearrange("p (c i j) -> p c j i", i=PACK, j=PACK)[:, h * n : (h + 1) * n, :, :]
+            copy(dst, raw[:].rearrange("p j (c i) -> p c j i", i=PACK))
+
+        def quantize(mx, grouped, a, b):
+            nc.vector.quantize_mx(out=mx[0][:, a:b].bitcast(FP8X4), scales=mx[1][:, a:b], in_=grouped[:, PACK * a : PACK * b])
+
+        def products(name, stationary, moving, tags):
+            share = PACK // len(tags)
+            banks = [psum.tile([P, share * S], F32, name="%s_bank%d" % (name, u), tag="bank%d" % u) for u in tags]
+            outs = [banks[t // share][:, (t % share) * S : (t % share + 1) * S] for t in range(PACK)]
+            for t in range(PACK):
+                cols = slice(t * P, (t + 1) * P)
+                nc.tensor.matmul_mx(out=outs[t], lhsT=stationary[0][:, cols].bitcast(FP8X4), lhsT_scale=stationary[1][:, cols],
+                                    rhs=moving[0][:].bitcast(FP8X4), rhs_scale=moving[1][:], start=True, stop=True)
+            return banks
+
+        def part(pairs, t, width=S):
+            return pairs[t // 2][:, (t % 2) * width : (t % 2 + 1) * width]
+
+        x_offs, x_two, x_cand = mx_tiles("x_offs", S), mx_tiles("x_two", S), mx_tiles("x_cand", C)
+        q1, q2, q3 = mx_tiles("q1", K), mx_tiles("q2", K), mx_tiles("q3", K)
+        qz, qz2 = mx_tiles("qz", S), mx_tiles("qz2", S)
+        g1 = keep.tile([P, PACK * K], BF16, name="g1", align_bytes=64)
+        g2 = keep.tile([P, PACK * K], BF16, name="g2", tag="reused", align_bytes=64)
+        g3 = keep.tile([P, PACK * K], BF16, name="g3", align_bytes=64)
+        z_bf = keep.tile([P, PACK * S], BF16, name="z_bf", align_bytes=64)
+        z2_bf = keep.tile([P, PACK * S], BF16, name="z2_bf", align_bytes=64)
+
+        deal_half(nc.scalar.copy, g1, w1_raw[0], 0)
+        deal_half(nc.scalar.copy, g1, w1_raw[1], 1)
+        pick_scales(x_offs, l_offs)
+        pick_scales(x_two, l_two)
+        quantize(q1, g1, 0, K)
+        pick_words(x_offs, l_offs)
+        pick_scales(x_cand, l_cand)
+
+        y_win = [keep.tile([P, 2 * S], F32, name="y_win%d" % t) for t in range(PACK)]
+        for t in range(PACK):
+            nc.gpsimd.memset(y_win[t][:, S:], 0.0)
+        y_banks = products("y", q1, x_offs, (0, 1, 2, 3))
+        for t in range(PACK):
+            nc.vector.tensor_copy(y_win[t][:, :S], y_banks[t][:])
+        pick_words(x_two, l_two)
+        deal_half(nc.vector.tensor_copy, g2, w2_raw[0], 0)
+        deal_half(nc.vector.tensor_copy, g2, w2_raw[1], 1)
+        pick_words(x_cand, l_cand)
+        quantize(q2, g2, 0, K)
+        d_banks = products("d", q2, x_two, (4, 5))
+        d_sb = [keep.tile([P, 2 * S], F32, name="d_sb%d" % u) for u in range(2)]
+
+        y_got = [[keep.tile([P, 2 * S], F32, name="y_n%d_%d" % (i + 1, u)) for u in range(2)] for i in range(3)]
+        for t in range(PACK):
+            for got, offsets in zip(y_got, (l_n1, l_n2, l_n3)):
+                nc.scalar.activation(part(got, t), y_win[t][:].indirect(offsets[:]), COPY)
+        upper = keep.tile([P, PACK * S], F32, name="upper", tag="reused", align_bytes=64)
+        lower = keep.tile([P, PACK * S], F32, name="lower", tag="reused_raw")
+        diff = keep.tile([P, PACK * S], F32, name="diff")
+        pa = [keep.tile([P, 2 * W], F32, name="pa%d" % u) for u in range(2)]
+        pb = [keep.tile([P, 2 * W], F32, name="pb%d" % u) for u in range(2)]
+        ra = [keep.tile([P, 2 * W], F32, name="ra%d" % u) for u in range(2)]
+        rb = [keep.tile([P, 2 * W], F32, name="rb%d" % u) for u in range(2)]
+
+        def maxima(u):
+            for t in (2 * u, 2 * u + 1):
+                nc.vector.tensor_tensor(upper[:, t * S : (t + 1) * S], y_banks[t][:], part(y_got[0], t), ALU.max)
+            nc.vector.tensor_tensor(lower[:, 2 * u * S : 2 * (u + 1) * S], y_got[1][u][:], y_got[2][u][:], ALU.max)
+
+        def difference(u):
+            nc.vector.tensor_tensor(diff[:, 2 * u * S : 2 * (u + 1) * S], upper[:, 2 * u * S : 2 * (u + 1) * S], lower[:, 2 * u * S : 2 * (u + 1) * S], ALU.subtract)
+
+        def pair_up(u):
+            nc.vector.tensor_tensor(ra[u][:], pa[u][:], pb[u][:], ALU.add)
+            nc.vector.tensor_tensor(rb[u][:], pa[u][:], pb[u][:], ALU.mult)
+
+        maxima(0)
+        nc.vector.tensor_copy(d_sb[0][:], d_banks[0][:])
+        difference(0)
+        nc.vector.tensor_copy(d_sb[1][:], d_banks[1][:])
+        for t in range(PACK):
+            nc.scalar.activation(part(pa, t, W), part(d_sb, t).indirect(l_n4[:]), COPY)
+            nc.scalar.activation(part(pb, t, W), part(d_sb, t).indirect(l_n5[:]), COPY)
+        maxima(1)
+        pair_up(0)
+        difference(1)
+        pair_up(1)
+        weave_half(nc.vector.tensor_copy, g3, w3_raw[0], 0)
+        nc.vector.tensor_tensor(
+            z_bf[:].rearrange("p (c i t) -> p c t i", i=PACK, t=PACK),
+            diff[:].rearrange("p (t c i) -> p c t i", i=PACK, t=PACK),
+            gn_sb[:].unsqueeze(1).unsqueeze(3).to_broadcast([P, S // PACK, PACK, PACK]),
+            ALU.mult,
+        )
+        weave_half(nc.vector.tensor_copy, g3, w3_raw[1], 1)
+        quantize(qz, z_bf, 0, S)
+
+        dt = [keep.tile([P, S], F32, name="dt%d" % t) for t in range(PACK)]
+
+        def put_back(u):
+            for values, offsets in ((ra, l_n4), (rb, l_n5)):
+                for t in (2 * u, 2 * u + 1):
+                    nc.scalar.activation(dt[t][:].indirect(offsets[:]), part(values, t, W), COPY)
+
+        def weigh(t):
+            nc.vector.tensor_scalar(z2_bf[:, t :: PACK], dt[t][:], gs_sb[:, t : t + 1], None, ALU.mult)
+
+        put_back(0)
+        weigh(0)
+        quantize(q3, g3, 0, K)
+        weigh(1)
+        a_banks = products("a", q3, qz, (0, 1, 2, 3))
+        a_sb = [keep.tile([P, S], F32, name="a_sb%d" % t) for t in range(PACK)]
+        for t in range(PACK):
+            nc.vector.tensor_copy(a_sb[t][:], a_banks[t][:])
+        put_back(1)
+        weigh(2)
+        weigh(3)
+        quantize(qz2, z2_bf, 0, S)
+        b_banks = products("b", x_cand, qz2, (6, 7, 4, 5))
+
+        a_got = []
+        for t in range(PACK):
+            got = keep.tile([P, W], F32, name="a_n6_%d" % t)
+            nc.scalar.activation(got[:], a_sb[t][:].indirect(l_n6[:]), COPY)
+            a_got.append(got)
+        mixed = []
+        for t in range(PACK):
+            b_sb = keep.tile([P, S], F32, name="b_sb%d" % t)
+            nc.vector.tensor_scalar(b_sb[:], b_banks[t][:], 0.0625, None, ALU.mult)
+            got = keep.tile([P, W], F32, name="b_n7_%d" % t)
+            nc.scalar.activation(got[:], b_sb[:].indirect(l_n7[:]), COPY)
+            ra2 = keep.tile([P, W], F32, name="ra2_%d" % t)
+            nc.vector.scalar_tensor_tensor(ra2[:], a_got[t][:], -0.5, got[:], ALU.mult, ALU.add)
+            mixed.append(ra2)
+        for t in range(PACK):
+            nc.scalar.activation(a_sb[t][:].indirect(l_n6[:]), mixed[t][:], COPY)
+            nc.sync.dma_start(out[t * P : (t + 1) * P, :], a_sb[t][:])

@@ -34,10 +34,10 @@ def tile_picked_tfcdputbmixbond_none_p_kernel(tc, x_words, x_scales, w1, w2, gn,
             nc.sync.dma_start(tile[:], src)
             return tile
 
-        def load_half(name, w, h):
-            raw = keep.tile([P, PACK, HALF], F32, name=name, tag="reused_raw" if name == "w2_1" else name)
-            nc.sync.dma_start(raw[:], w.rearrange("(p j) c -> p j c", j=PACK)[:, :, h * HALF : (h + 1) * HALF])
-            return raw
+        def load_weight(name, w, tag):
+            raw = keep.tile([P, PACK, K], F32, name=name, tag=tag)
+            nc.sync.dma_start(raw[:], w.rearrange("(p j) c -> p j c", j=PACK))
+            return [raw[:, :, h * HALF : (h + 1) * HALF] for h in range(2)]
 
         def load_gain(name, g):
             tile = keep.tile([P, PACK], F32, name=name)
@@ -49,22 +49,21 @@ def tile_picked_tfcdputbmixbond_none_p_kernel(tc, x_words, x_scales, w1, w2, gn,
         xw = keep.tile([P, T], I32, name="xw")
 
         l_offs = load_list("l_offs", offs)
-        l_two = load_list("l_two", two)
-        w1_raw = [load_half("w1_0", w1, 0)]
+        w1_raw = load_weight("w1_raw", w1, "w1_raw")
         for q in range(4):
             nc.sync.dma_start(xs[32 * q : 32 * q + 4, :].bitcast(I32), x_scales[0, 4 * q : 4 * q + 4, :].bitcast(I32))
-        w1_raw.append(load_half("w1_1", w1, 1))
-        l_cand = load_list("l_cand", cand)
         nc.sync.dma_start(xw[:], x_words[0].rearrange("p c r -> p (c r)").bitcast(I32))
         l_n1 = load_list("l_n1", n1)
         l_n2 = load_list("l_n2", n2)
         l_n3 = load_list("l_n3", n3)
+        l_two = load_list("l_two", two)
+        w2_raw = load_weight("w2_raw", w2, "reused_raw")
+        l_cand = load_list("l_cand", cand)
         gn_sb = load_gain("gn_sb", gn)
-        w2_raw = [load_half("w2_%d" % h, w2, h) for h in range(2)]
         l_n4 = load_list("l_n4", n4)
         l_n5 = load_list("l_n5", n5)
         gs_sb = load_gain("gs_sb", gs)
-        w3_raw = [load_half("w3_%d" % h, w3, h) for h in range(2)]
+        w3_raw = load_weight("w3_raw", w3, "w3_raw")
         l_n6 = load_list("l_n6", n6)
         l_n7 = load_list("l_n7", n7)
 
@@ -79,15 +78,18 @@ def tile_picked_tfcdputbmixbond_none_p_kernel(tc, x_words, x_scales, w1, w2, gn,
         def pick_words(picked, offsets):
             nc.vector.tensor_copy(picked[0][:], xw[:].bitcast(U32).indirect(offsets[:]))
 
+        def gpsimd_round(dst, src):
+            nc.gpsimd.tensor_scalar(dst, src, 1.0, 0.0, ALU.mult, ALU.add)
+
         def deal_half(copy, grouped, raw, h):
             m = HALF // PACK
             dst = grouped[:].rearrange("p (t m j) -> p m t j", t=PACK, j=PACK)[:, h * m : (h + 1) * m, :, :]
-            copy(dst, raw[:].rearrange("p j (m t) -> p m t j", t=PACK))
+            copy(dst, raw.rearrange("p j (m t) -> p m t j", t=PACK))
 
         def weave_half(copy, grouped, raw, h):
             n = HALF // PACK
             dst = grouped[:].rearrange("p (c i j) -> p c j i", i=PACK, j=PACK)[:, h * n : (h + 1) * n, :, :]
-            copy(dst, raw[:].rearrange("p j (c i) -> p c j i", i=PACK))
+            copy(dst, raw.rearrange("p j (c i) -> p c j i", i=PACK))
 
         def quantize(mx, grouped, a, b):
             nc.vector.quantize_mx(out=mx[0][:, a:b].bitcast(FP8X4), scales=mx[1][:, a:b], in_=grouped[:, PACK * a : PACK * b])
@@ -115,24 +117,25 @@ def tile_picked_tfcdputbmixbond_none_p_kernel(tc, x_words, x_scales, w1, w2, gn,
         z2_bf = keep.tile([P, PACK * S], BF16, name="z2_bf", align_bytes=64)
 
         deal_half(nc.scalar.copy, g1, w1_raw[0], 0)
-        deal_half(nc.scalar.copy, g1, w1_raw[1], 1)
+        deal_half(nc.vector.tensor_copy, g1, w1_raw[1], 1)
         pick_scales(x_offs, l_offs)
-        pick_scales(x_two, l_two)
         quantize(q1, g1, 0, K)
         pick_words(x_offs, l_offs)
-        pick_scales(x_cand, l_cand)
+        pick_scales(x_two, l_two)
 
         y_win = [keep.tile([P, 2 * S], F32, name="y_win%d" % t) for t in range(PACK)]
         for t in range(PACK):
             nc.gpsimd.memset(y_win[t][:, S:], 0.0)
         y_banks = products("y", q1, x_offs, (0, 1, 2, 3))
-        for t in range(PACK):
+        nc.scalar.copy(y_win[0][:, :S], y_banks[0][:])
+        for t in range(1, PACK):
             nc.vector.tensor_copy(y_win[t][:, :S], y_banks[t][:])
         pick_words(x_two, l_two)
         deal_half(nc.vector.tensor_copy, g2, w2_raw[0], 0)
         deal_half(nc.vector.tensor_copy, g2, w2_raw[1], 1)
-        pick_words(x_cand, l_cand)
         quantize(q2, g2, 0, K)
+        pick_scales(x_cand, l_cand)
+        pick_words(x_cand, l_cand)
         d_banks = products("d", q2, x_two, (4, 5))
         d_sb = [keep.tile([P, 2 * S], F32, name="d_sb%d" % u) for u in range(2)]
 
@@ -171,14 +174,14 @@ def tile_picked_tfcdputbmixbond_none_p_kernel(tc, x_words, x_scales, w1, w2, gn,
         pair_up(0)
         difference(1)
         pair_up(1)
-        weave_half(nc.vector.tensor_copy, g3, w3_raw[0], 0)
+        weave_half(gpsimd_round, g3, w3_raw[0], 0)
         nc.vector.tensor_tensor(
             z_bf[:].rearrange("p (c i t) -> p c t i", i=PACK, t=PACK),
             diff[:].rearrange("p (t c i) -> p c t i", i=PACK, t=PACK),
             gn_sb[:].unsqueeze(1).unsqueeze(3).to_broadcast([P, S // PACK, PACK, PACK]),
             ALU.mult,
         )
-        weave_half(nc.vector.tensor_copy, g3, w3_raw[1], 1)
+        weave_half(gpsimd_round, g3, w3_raw[1], 1)
         quantize(qz, z_bf, 0, S)
 
         dt = [keep.tile([P, S], F32, name="dt%d" % t) for t in range(PACK)]
@@ -188,8 +191,8 @@ def tile_picked_tfcdputbmixbond_none_p_kernel(tc, x_words, x_scales, w1, w2, gn,
                 for t in (2 * u, 2 * u + 1):
                     nc.scalar.activation(dt[t][:].indirect(offsets[:]), part(values, t, W), COPY)
 
-        def weigh(t):
-            nc.vector.tensor_scalar(z2_bf[:, t :: PACK], dt[t][:], gs_sb[:, t : t + 1], None, ALU.mult)
+        def weigh(t, a=0, b=S):
+            nc.vector.tensor_scalar(z2_bf[:, PACK * a + t : PACK * b : PACK], dt[t][:, a:b], gs_sb[:, t : t + 1], None, ALU.mult)
 
         put_back(0)
         weigh(0)
@@ -201,9 +204,15 @@ def tile_picked_tfcdputbmixbond_none_p_kernel(tc, x_words, x_scales, w1, w2, gn,
             nc.vector.tensor_copy(a_sb[t][:], a_banks[t][:])
         put_back(1)
         weigh(2)
-        weigh(3)
-        quantize(qz2, z2_bf, 0, S)
-        b_banks = products("b", x_cand, qz2, (6, 7, 4, 5))
+        weigh(3, 0, W)
+        weigh(3, W, S)
+        quantize(qz2, z2_bf, 0, W)
+        quantize(qz2, z2_bf, W, S)
+        b_banks = [psum.tile([P, S], F32, name="b_bank%d" % u, tag="bank%d" % u) for u in (6, 7, 4, 5)]
+        for t, a, b in [(0, 0, W), (0, W, S)] + [(t, 0, S) for t in range(1, PACK)]:
+            cols = slice(t * P, (t + 1) * P)
+            nc.tensor.matmul_mx(out=b_banks[t][:, a:b], lhsT=x_cand[0][:, cols].bitcast(FP8X4), lhsT_scale=x_cand[1][:, cols],
+                                rhs=qz2[0][:, a:b].bitcast(FP8X4), rhs_scale=qz2[1][:, a:b], start=True, stop=True)
 
         a_got = []
         for t in range(PACK):

from contextlib import ExitStack

import concourse.mybir as mybir

F32 = mybir.dt.float32
BF16 = mybir.dt.bfloat16
I32 = mybir.dt.int32
U32 = mybir.dt.uint32
U16 = mybir.dt.uint16
U8 = mybir.dt.uint8
FP8X4 = mybir.dt.float8_e4m3fn_x4
ALU = mybir.AluOpType
COPY = mybir.ActivationFunctionType.Copy

P = 128
PACK = 4
K = 512
T = 2048
S = 256
W = 128
C = 512
HALF = K // 2
FLOPS = 4 * 2 * K * K * S


def tile_picked_tfcdputbmixbond_none_p_kernel(tc, x_words, x_scales, w1, w2, gn, w3, gs, offs, two, n1, n2, n3, n4, n5, cand, n6, n7, out):
    nc = tc.nc
    with ExitStack() as ctx:
        keep = ctx.enter_context(tc.tile_pool(name="keep", bufs=1))
        psum = ctx.enter_context(tc.psum_pool(name="psum", bufs=1))

        def load_list(name, src):
            tile = keep.tile(list(src.shape), U16, name=name)
            nc.sync.dma_start(tile[:], src)
            return tile

        def load_weight(name, w, tag):
            raw = keep.tile([P, PACK, K], F32, name=name, tag=tag)
            nc.sync.dma_start(raw[:], w.rearrange("(p j) c -> p j c", j=PACK))
            return [raw[:, :, h * HALF : (h + 1) * HALF] for h in range(2)]

        def load_gain(name, g):
            tile = keep.tile([P, PACK], F32, name=name)
            nc.sync.dma_start(tile[:], g.rearrange("(p t) o -> p (t o)", t=PACK))
            return tile

        xs = keep.tile([P, T], U8, name="xs")
        nc.gpsimd.memset(xs[:].bitcast(I32), 0)
        xw = keep.tile([P, T], I32, name="xw")

        l_offs = load_list("l_offs", offs)
        w1_raw = load_weight("w1_raw", w1, "w1_raw")
        for q in range(4):
            nc.sync.dma_start(xs[32 * q : 32 * q + 4, :].bitcast(I32), x_scales[0, 4 * q : 4 * q + 4, :].bitcast(I32))
        nc.sync.dma_start(xw[:], x_words[0].rearrange("p c r -> p (c r)").bitcast(I32))
        l_n1 = load_list("l_n1", n1)
        l_n2 = load_list("l_n2", n2)
        l_n3 = load_list("l_n3", n3)
        l_two = load_list("l_two", two)
        w2_raw = load_weight("w2_raw", w2, "reused_raw")
        l_cand = load_list("l_cand", cand)
        gn_sb = load_gain("gn_sb", gn)
        l_n4 = load_list("l_n4", n4)
        l_n5 = load_list("l_n5", n5)
        gs_sb = load_gain("gs_sb", gs)
        w3_raw = load_weight("w3_raw", w3, "w3_raw")
        l_n6 = load_list("l_n6", n6)
        l_n7 = load_list("l_n7", n7)

        def mx_tiles(name, width):
            words = keep.tile([P, width], U32, name=name + "_words", align_bytes=64)
            scales = keep.tile([P, width], U8, name=name + "_scales", align_bytes=64)
            return words, scales

        def pick_scales(picked, offsets):
            nc.vector.tensor_copy(picked[1][:], xs[:].indirect(offsets[:]))

        def pick_words(picked, offsets):
            nc.vector.tensor_copy(picked[0][:], xw[:].bitcast(U32).indirect(offsets[:]))

        def gpsimd_round(dst, src):
            nc.gpsimd.tensor_scalar(dst, src, 1.0, 0.0, ALU.mult, ALU.add)

        def deal_half(copy, grouped, raw, h):
            m = HALF // PACK
            dst = grouped[:].rearrange("p (t m j) -> p m t j", t=PACK, j=PACK)[:, h * m : (h + 1) * m, :, :]
            copy(dst, raw.rearrange("p j (m t) -> p m t j", t=PACK))

        def weave_half(copy, grouped, raw, h):
            n = HALF // PACK
            dst = grouped[:].rearrange("p (c i j) -> p c j i", i=PACK, j=PACK)[:, h * n : (h + 1) * n, :, :]
            copy(dst, raw.rearrange("p j (c i) -> p c j i", i=PACK))

        def quantize(mx, grouped, a, b):
            nc.vector.quantize_mx(out=mx[0][:, a:b].bitcast(FP8X4), scales=mx[1][:, a:b], in_=grouped[:, PACK * a : PACK * b])

        def products(name, stationary, moving, tags):
            share = PACK // len(tags)
            banks = [psum.tile([P, share * S], F32, name="%s_bank%d" % (name, u), tag="bank%d" % u) for u in tags]
            outs = [banks[t // share][:, (t % share) * S : (t % share + 1) * S] for t in range(PACK)]
            for t in range(PACK):
                cols = slice(t * P, (t + 1) * P)
                nc.tensor.matmul_mx(out=outs[t], lhsT=stationary[0][:, cols].bitcast(FP8X4), lhsT_scale=stationary[1][:, cols],
                                    rhs=moving[0][:].bitcast(FP8X4), rhs_scale=moving[1][:], start=True, stop=True)
            return banks

        def part(pairs, t, width=S):
            return pairs[t // 2][:, (t % 2) * width : (t % 2 + 1) * width]

        x_offs, x_two, x_cand = mx_tiles("x_offs", S), mx_tiles("x_two", S), mx_tiles("x_cand", C)
        q1, q2, q3 = mx_tiles("q1", K), mx_tiles("q2", K), mx_tiles("q3", K)
        qz, qz2 = mx_tiles("qz", S), mx_tiles("qz2", S)
        g1 = keep.tile([P, PACK * K], BF16, name="g1", align_bytes=64)
        g2 = keep.tile([P, PACK * K], BF16, name="g2", tag="reused", align_bytes=64)
        g3 = keep.tile([P, PACK * K], BF16, name="g3", align_bytes=64)
        z_bf = keep.tile([P, PACK * S], BF16, name="z_bf", align_bytes=64)
        z2_bf = keep.tile([P, PACK * S], BF16, name="z2_bf", align_bytes=64)

        deal_half(nc.scalar.copy, g1, w1_raw[0], 0)
        deal_half(nc.vector.tensor_copy, g1, w1_raw[1], 1)
        pick_scales(x_offs, l_offs)
        quantize(q1, g1, 0, K)
        pick_words(x_offs, l_offs)
        pick_scales(x_two, l_two)

        y_win = [keep.tile([P, 2 * S], F32, name="y_win%d" % t) for t in range(PACK)]
        for t in range(PACK):
            nc.gpsimd.memset(y_win[t][:, S:], 0.0)
        y_banks = products("y", q1, x_offs, (0, 1, 2, 3))
        nc.scalar.copy(y_win[0][:, :S], y_banks[0][:])
        for t in range(1, PACK):
            nc.vector.tensor_copy(y_win[t][:, :S], y_banks[t][:])
        pick_words(x_two, l_two)
        deal_half(nc.vector.tensor_copy, g2, w2_raw[0], 0)
        deal_half(nc.vector.tensor_copy, g2, w2_raw[1], 1)
        quantize(q2, g2, 0, K)
        pick_scales(x_cand, l_cand)
        pick_words(x_cand, l_cand)
        d_banks = products("d", q2, x_two, (4, 5))
        d_sb = [keep.tile([P, 2 * S], F32, name="d_sb%d" % u) for u in range(2)]

        y_got = [[keep.tile([P, 2 * S], F32, name="y_n%d_%d" % (i + 1, u)) for u in range(2)] for i in range(3)]
        for t in range(PACK):
            for got, offsets in zip(y_got, (l_n1, l_n2, l_n3)):
                nc.scalar.activation(part(got, t), y_win[t][:].indirect(offsets[:]), COPY)
        upper = keep.tile([P, PACK * S], F32, name="upper", tag="reused", align_bytes=64)
        lower = keep.tile([P, PACK * S], F32, name="lower", tag="reused_raw")
        diff = keep.tile([P, PACK * S], F32, name="diff")
        pa = [keep.tile([P, 2 * W], F32, name="pa%d" % u) for u in range(2)]
        pb = [keep.tile([P, 2 * W], F32, name="pb%d" % u) for u in range(2)]
        ra = [keep.tile([P, 2 * W], F32, name="ra%d" % u) for u in range(2)]
        rb = [keep.tile([P, 2 * W], F32, name="rb%d" % u) for u in range(2)]

        def maxima(u):
            for t in (2 * u, 2 * u + 1):
                nc.vector.tensor_tensor(upper[:, t * S : (t + 1) * S], y_banks[t][:], part(y_got[0], t), ALU.max)
            nc.vector.tensor_tensor(lower[:, 2 * u * S : 2 * (u + 1) * S], y_got[1][u][:], y_got[2][u][:], ALU.max)

        def difference(u):
            nc.vector.tensor_tensor(diff[:, 2 * u * S : 2 * (u + 1) * S], upper[:, 2 * u * S : 2 * (u + 1) * S], lower[:, 2 * u * S : 2 * (u + 1) * S], ALU.subtract)

        def pair_up(u):
            nc.vector.tensor_tensor(ra[u][:], pa[u][:], pb[u][:], ALU.add)
            nc.vector.tensor_tensor(rb[u][:], pa[u][:], pb[u][:], ALU.mult)

        maxima(0)
        nc.vector.tensor_copy(d_sb[0][:], d_banks[0][:])
        difference(0)
        nc.vector.tensor_copy(d_sb[1][:], d_banks[1][:])
        for t in range(PACK):
            nc.scalar.activation(part(pa, t, W), part(d_sb, t).indirect(l_n4[:]), COPY)
            nc.scalar.activation(part(pb, t, W), part(d_sb, t).indirect(l_n5[:]), COPY)
        maxima(1)
        pair_up(0)
        difference(1)
        pair_up(1)
        weave_half(gpsimd_round, g3, w3_raw[0], 0)
        nc.vector.tensor_tensor(
            z_bf[:].rearrange("p (c i t) -> p c t i", i=PACK, t=PACK),
            diff[:].rearrange("p (t c i) -> p c t i", i=PACK, t=PACK),
            gn_sb[:].unsqueeze(1).unsqueeze(3).to_broadcast([P, S // PACK, PACK, PACK]),
            ALU.mult,
        )
        weave_half(gpsimd_round, g3, w3_raw[1], 1)
        quantize(qz, z_bf, 0, S)

        dt = [keep.tile([P, S], F32, name="dt%d" % t) for t in range(PACK)]

        def put_back(u):
            for values, offsets in ((ra, l_n4), (rb, l_n5)):
                for t in (2 * u, 2 * u + 1):
                    nc.scalar.activation(dt[t][:].indirect(offsets[:]), part(values, t, W), COPY)

        def weigh(t, a=0, b=S):
            nc.vector.tensor_scalar(z2_bf[:, PACK * a + t : PACK * b : PACK], dt[t][:, a:b], gs_sb[:, t : t + 1], None, ALU.mult)

        put_back(0)
        weigh(0)
        quantize(q3, g3, 0, K)
        weigh(1)
        a_banks = products("a", q3, qz, (0, 1, 2, 3))
        a_sb = [keep.tile([P, S], F32, name="a_sb%d" % t) for t in range(PACK)]
        for t in range(PACK):
            nc.vector.tensor_copy(a_sb[t][:], a_banks[t][:])
        put_back(1)
        weigh(2)
        weigh(3, 0, W)
        weigh(3, W, S)
        quantize(qz2, z2_bf, 0, W)
        quantize(qz2, z2_bf, W, S)
        b_banks = [psum.tile([P, S], F32, name="b_bank%d" % u, tag="bank%d" % u) for u in (6, 7, 4, 5)]
        for t, a, b in [(0, 0, W), (0, W, S)] + [(t, 0, S) for t in range(1, PACK)]:
            cols = slice(t * P, (t + 1) * P)
            nc.tensor.matmul_mx(out=b_banks[t][:, a:b], lhsT=x_cand[0][:, cols].bitcast(FP8X4), lhsT_scale=x_cand[1][:, cols],
                                rhs=qz2[0][:, a:b].bitcast(FP8X4), rhs_scale=qz2[1][:, a:b], start=True, stop=True)

        a_got = []
        for t in range(PACK):
            got = keep.tile([P, W], F32, name="a_n6_%d" % t)
            nc.scalar.activation(got[:], a_sb[t][:].indirect(l_n6[:]), COPY)
            a_got.append(got)
        mixed = []
        for t in range(PACK):
            b_sb = keep.tile([P, S], F32, name="b_sb%d" % t)
            nc.vector.tensor_scalar(b_sb[:], b_banks[t][:], 0.0625, None, ALU.mult)
            got = keep.tile([P, W], F32, name="b_n7_%d" % t)
            nc.scalar.activation(got[:], b_sb[:].indirect(l_n7[:]), COPY)
            ra2 = keep.tile([P, W], F32, name="ra2_%d" % t)
            nc.vector.scalar_tensor_tensor(ra2[:], a_got[t][:], -0.5, got[:], ALU.mult, ALU.add)
            mixed.append(ra2)
        for t in range(PACK):
            nc.scalar.activation(a_sb[t][:].indirect(l_n6[:]), mixed[t][:], COPY)
            nc.sync.dma_start(out[t * P : (t + 1) * P, :], a_sb[t][:])
